import numpy as np
import ml_dtypes


def mxq(x, axis, fmt="e4m3"):
    dtype, down = {"e4m3": (ml_dtypes.float8_e4m3fn, 7), "e5m2": (ml_dtypes.float8_e5m2, 14)}[fmt]
    v = np.moveaxis(np.asarray(x, np.float32).astype(ml_dtypes.bfloat16).astype(np.float64), axis, -1)
    blocks = v.reshape(v.shape[:-1] + (-1, 32))
    amax = np.abs(blocks).max(-1, keepdims=True)
    byte = np.maximum(np.where(amax > 0, np.frexp(amax)[1] - 1 + 127, 0) - down, 1)
    scale = np.exp2(byte - 127.0)
    codes = (blocks / scale).astype(np.float32).astype(dtype).astype(np.float64)
    return np.moveaxis((codes * scale).reshape(v.shape), -1, axis)


WIDE = False


def mx_kscale(k):
    if not WIDE:
        return np.ones(k)
    levels = np.array([10, -10, 5, -5, 0])
    if k % 512:
        return np.exp2(np.random.permutation(np.resize(levels, k // 32))).repeat(32)
    a = np.empty((k // 512, 16))
    for p in range(k // 512):
        a[p, :8] = np.random.permutation(np.resize(levels, 8))
        for g in range(8):
            far = levels[np.abs(levels - a[p, g]) >= 10]
            a[p, g + 8] = far[np.random.randint(len(far))]
    return np.exp2(a.ravel()).repeat(32)


def f64(x):
    return np.asarray(x).astype(np.float64)


def striped(idx):
    return np.tile(idx.reshape(-1, 16).T, (8, 1)).astype(np.uint16)


def unstriped(offs):
    return offs[:16].T.reshape(-1).astype(np.int64)


def striped8(idx):
    return np.concatenate([x.reshape(-1, 16).T for x in idx]).astype(np.uint16)


def runs(offs, k):
    lists = np.stack([offs[16 * r : 16 * r + 16].T.reshape(-1) for r in range(8)]).astype(np.int64)
    return lists[np.arange(k) % 512 // 64]


def pack_weight(w):
    k, n = w.shape
    w = f64(np.asarray(w, np.float32).astype(ml_dtypes.bfloat16)).reshape(k // 32, 32, n)
    amax = np.abs(w).max(1)
    byte = np.clip(np.where(amax > 0, np.frexp(amax)[1] - 1 + 127 - 7, 1), 1, 254)
    scaled = (w * np.exp2(127.0 - byte)[:, None, :]).reshape(k, n).astype(np.float32)
    words = np.ascontiguousarray(scaled.reshape(k // 512, 128, 4, n).transpose(0, 1, 3, 2)).astype(ml_dtypes.float8_e4m3fn).view(np.uint8)
    return words, np.ascontiguousarray(byte.astype(np.uint8).reshape(k // 512, 16, n))


def unpack_weight(words, scales):
    g, p, n, _ = words.shape
    vals = np.ascontiguousarray(words).view(ml_dtypes.float8_e4m3fn).astype(np.float64) * np.repeat(np.exp2(scales.astype(np.float64) - 127.0), 8, axis=1)[..., None]
    return vals.transpose(0, 1, 3, 2).reshape(g * 512, n)


def sigmoid(v):
    return 1.0 / (1.0 + np.exp(-np.maximum(v, -700.0)))

def planes(y):
    n, m = y.shape
    v = y.astype(np.float32).astype(ml_dtypes.bfloat16).astype(np.float64).reshape(n // 32, 32, m)
    top = np.abs(v).max(1)
    byte = np.clip(np.where(top > 0, np.frexp(top)[1] - 1 + 127 - 7, 1), 1, 254)
    codes = (v * np.exp2(127.0 - byte)[:, None, :]).reshape(n, m).astype(np.float32).astype(ml_dtypes.float8_e4m3fn).view(np.uint8)
    words = codes.reshape(n // 512, 128, 4, m).transpose(0, 1, 3, 2)
    return np.ascontiguousarray(words), np.ascontiguousarray(byte.astype(np.uint8).reshape(n // 512, 16, m))


K, T, S, N, H, W = 512, 2048, 512, 512, 512, 256


def setup_inputs():
    n = np.random.standard_normal
    s = mx_kscale(K)[:, None]
    u = mx_kscale(S)
    packed_xT = pack_weight(n((K, T)) * s)
    perm = np.stack([np.random.permutation(H) for _ in range(8)])
    return {
        "x_words": packed_xT[0],
        "x_scales": packed_xT[1],
        "wa": (n((K, H)) / np.sqrt(K) / s).astype(np.float32),
        "wb": (n((K, N)) / np.sqrt(K) / s).astype(np.float32),
        "gt": (np.random.uniform(0.5, 1.5, (S, 1)) * u[:, None]).astype(np.float32),
        "gi": (np.random.uniform(0.5, 1.5, (S, 1)) / u[:, None]).astype(np.float32),
        "offs": striped(np.random.permutation(T)[:S]),
        "two": striped(np.random.permutation(T)[:S]),
        "n1": striped8(perm[:, :W]),
        "n2": striped8(perm[:, W:]),
        "n3": striped8(np.stack([np.random.permutation(N) for _ in range(8)])),
        "n4": striped8(np.stack([np.random.permutation(N) for _ in range(8)])),
    }


def reference(x_words, x_scales, wa, wb, gt, gi, offs, two, n1, n2, n3, n4):
    xq = unpack_weight(x_words, x_scales)[:, unstriped(offs)]
    a = xq.T @ mxq(f64(wa), 0, "e4m3")
    pa = a[np.arange(S)[:, None], runs(n1, S)]
    pb = a[np.arange(S)[:, None], runs(n2, S)]
    rb = pa - pb
    ra = 0.75 * (pa + pb)
    ds = np.zeros((S, H))
    ds[np.arange(S)[:, None], runs(n1, S)] = ra
    dt = ds.copy()
    dt[np.arange(S)[:, None], runs(n2, S)] = rb
    z = f64(gt) * dt
    x_two = unpack_weight(x_words, x_scales)[:, unstriped(two)]
    b = x_two.T @ mxq(f64(wb), 0, "e4m3")
    z2 = f64(gi) * b
    cv = 0.0625 * ((mxq(z, 0, "e4m3").T @ mxq(z2, 0, "e4m3")))
    out_0 = (cv - (cv[np.arange(H)[:, None], runs(n3, H)])) * (sigmoid(cv[np.arange(H)[:, None], runs(n4, H)]))
    return (out_0,) + planes(out_0)

@@ -1,0 +1,252 @@
+from contextlib import ExitStack
+
+import concourse.mybir as mybir
+from concourse.masks import make_identity
+
+F32 = mybir.dt.float32
+BF16 = mybir.dt.bfloat16
+U32 = mybir.dt.uint32
+I32 = mybir.dt.int32
+U16 = mybir.dt.uint16
+U8 = mybir.dt.uint8
+FP8X4 = mybir.dt.float8_e4m3fn_x4
+ALU = mybir.AluOpType
+ACT = mybir.ActivationFunctionType
+
+P = 128
+PACK = 4
+T = 2048
+D = 512
+W = 256
+QUADS = 4
+FLOPS = 3 * 2 * D * D * D
+
+
+def tile_picked_momhaargdif_none_po_kernel(
+    tc, x_words, x_scales, wa, wb, gt, gi, offs, two, n1, n2, n3, n4, out_0, out_1, out_2
+):
+    nc = tc.nc
+    with ExitStack() as ctx:
+        keep = ctx.enter_context(tc.tile_pool(name="keep", bufs=1))
+        psum = ctx.enter_context(tc.psum_pool(name="psum", bufs=4))
+
+        def sb(name, shape, dtype, tag=None):
+            return keep.tile(shape, dtype, name=name, tag=tag or name, align_bytes=64)
+
+        def load_list(name, src):
+            tile = sb(name, list(src.shape), U16)
+            nc.sync.dma_start(tile[:], src)
+            return tile
+
+        def load_weight_half(name, w, h):
+            tile = sb(name, [P, PACK, W], F32)
+            nc.sync.dma_start(tile[:], w.rearrange("(p j) c -> p j c", j=PACK)[:, :, h * W : (h + 1) * W])
+            return tile
+
+        def mx(out, lhs_words, lhs_scales, t, rhs_words, rhs_scales):
+            cols = slice(t * P, (t + 1) * P)
+            nc.tensor.matmul_mx(
+                out=out[:],
+                lhsT=lhs_words[:, cols].bitcast(FP8X4),
+                lhsT_scale=lhs_scales[:, cols],
+                rhs=rhs_words[:].bitcast(FP8X4),
+                rhs_scale=rhs_scales[:],
+                start=True,
+                stop=True,
+            )
+
+        def quantize(words, scales, grouped, c0, c1):
+            nc.vector.quantize_mx(
+                out=words[:, c0:c1].bitcast(FP8X4),
+                scales=scales[:, c0:c1],
+                in_=grouped[:, c0:c1, :].rearrange("p c j -> p (c j)"),
+            )
+
+        def lines(ap, pattern):
+            return ap.rearrange(pattern, i=4)
+
+        xs = sb("xs", [P, T], U8)
+        nc.vector.memset(xs[:].bitcast(I32), 0)
+        gate_rows = sb("gate_rows", [P, P], F32)
+        nc.gpsimd.memset(gate_rows[:], 0.0)
+        factor = sb("factor", [P, W], F32)
+        nc.gpsimd.memset(factor[:], -0.75)
+        ident = sb("ident", [P, P], F32)
+        make_identity(nc, ident[:])
+
+        offs_l = load_list("offs_l", offs)
+        two_l = load_list("two_l", two)
+        for q in range(QUADS):
+            nc.sync.dma_start(xs[32 * q : 32 * q + 4, :].bitcast(I32), x_scales[0, 4 * q : 4 * q + 4, :].bitcast(I32))
+        warm = sb("warm", [P, 1], F32)
+        nc.scalar.activation(warm[:], factor[:, 0:1], ACT.Sigmoid)
+        xw = sb("xw", [P, T], I32)
+        nc.sync.dma_start(xw[:], x_words[0].rearrange("p n r -> p (n r)").bitcast(I32))
+        wa_raw = [load_weight_half(f"wa_raw{h}", wa, h) for h in range(2)]
+        n1_l = load_list("n1_l", n1)
+        n2_l = load_list("n2_l", n2)
+        for g, vec in enumerate((gt, gi)):
+            nc.sync.dma_start(
+                gate_rows[PACK * g : PACK * (g + 1), :].rearrange("t (b r) -> t b r", r=8),
+                vec.rearrange("(b t r) o -> t b (r o)", t=PACK, r=8),
+            )
+        wb_raw = [load_weight_half(f"wb_raw{h}", wb, h) for h in range(2)]
+        n3_l = load_list("n3_l", n3)
+        n4_l = load_list("n4_l", n4)
+
+        def pick_scales(name, lst):
+            picked = sb(name + "_picked", [P, D], U8)
+            nc.vector.tensor_copy(picked[:], xs[:].indirect(lst[:]))
+            dealt = sb(name, [P, D], U8)
+            nc.vector.tensor_copy(
+                dealt[:].bitcast(I32).rearrange("p (t b w) -> p t b w", t=PACK, w=2),
+                picked[:].bitcast(I32).rearrange("p (b t w) -> p t b w", t=PACK, w=2),
+            )
+            return dealt
+
+        def pick_words(name, lst):
+            dealt = sb(name, [P, D], U32)
+            nc.vector.tensor_copy(
+                dealt[:].rearrange("p (t b r) -> p b t r", t=PACK, r=8), xw[:].bitcast(U32).indirect(lst[:])
+            )
+            return dealt
+
+        def group_weight(name, raw):
+            grouped = sb(name, [P, D, PACK], BF16)
+            for h in range(2):
+                nc.scalar.copy(
+                    lines(grouped[:, h * W : (h + 1) * W, :], "p (c i) j -> p c j i"),
+                    lines(raw[h][:], "p j (c i) -> p c j i"),
+                )
+            return grouped
+
+        xa_scales = pick_scales("xa_scales", offs_l)
+        xb_scales = pick_scales("xb_scales", two_l)
+        xa_words = pick_words("xa_words", offs_l)
+        xb_words = pick_words("xb_words", two_l)
+        wa_grouped = sb("wa_grouped", [P, D, PACK], BF16)
+        wa_words = sb("wa_words", [P, D], U32)
+        wa_scales = sb("wa_scales", [P, D], U8)
+        for copy, h, c0, c1 in (
+            (nc.scalar.copy, 0, 0, W),
+            (nc.scalar.copy, 1, 0, P),
+            (nc.vector.tensor_copy, 1, P, W),
+        ):
+            copy(
+                lines(wa_grouped[:, h * W + c0 : h * W + c1, :], "p (c i) j -> p c j i"),
+                lines(wa_raw[h][:, :, c0:c1], "p j (c i) -> p c j i"),
+            )
+        for h in range(2):
+            quantize(wa_words, wa_scales, wa_grouped, h * W, (h + 1) * W)
+
+        neg_a = []
+        for t in range(PACK):
+            acc = psum.tile([P, D], F32, name="acc", tag="acc")
+            mx(acc, xa_words, xa_scales, t, wa_words, wa_scales)
+            window = sb(f"neg_a{t}", [P, D], F32)
+            nc.scalar.activation(window[:], acc[:], ACT.Copy, scale=-1.0)
+            neg_a.append(window)
+
+        turned = psum.tile([P, P], F32, name="turned", tag="side")
+        nc.tensor.transpose(turned[:], gate_rows[:], ident[:])
+        gates = sb("gates", [P, 2 * PACK], F32)
+        nc.scalar.copy(gates[:], turned[:, 0 : 2 * PACK])
+
+        z2_planes = sb("z2_planes", [P, PACK, D], BF16, tag="planes")
+        neg_sum = [sb(f"neg_sum{t}", [P, W], F32) for t in range(PACK)]
+        two_pa = [sb(f"two_pa{t}", [P, W], F32) for t in range(PACK)]
+        dt = [sb(f"dt{t}", [P, D], F32) for t in range(PACK)]
+
+        def haar(pair, neg_pa):
+            for t in pair:
+                nc.vector.tensor_copy(neg_pa[:, t % 2, :], neg_a[t][:].indirect(n1_l[:]))
+                nc.scalar.activation(two_pa[t][:], neg_pa[:, t % 2, :], ACT.Copy, scale=-2.0)
+            for t in pair:
+                nc.vector.tensor_tensor(neg_sum[t][:], neg_a[t][:].indirect(n2_l[:]), neg_pa[:, t % 2, :], ALU.add)
+            for t in pair:
+                nc.vector.tensor_tensor(dt[t][:].indirect(n1_l[:]), neg_sum[t][:], factor[:], ALU.mult)
+            for t in pair:
+                nc.vector.tensor_tensor(dt[t][:].indirect(n2_l[:]), neg_sum[t][:], two_pa[t][:], ALU.add)
+
+        haar((0, 1), sb("neg_pa01", [P, 2, W], F32))
+        wb_grouped = group_weight("wb_grouped", wb_raw)
+        wb_words = sb("wb_words", [P, D], U32)
+        wb_scales = sb("wb_scales", [P, D], U8)
+        quantize(wb_words, wb_scales, wb_grouped, 0, D)
+        for t in range(PACK):
+            side = psum.tile([P, D], F32, name="side", tag="side")
+            mx(side, xb_words, xb_scales, t, wb_words, wb_scales)
+            nc.scalar.activation(z2_planes[:, t, :], side[:], ACT.Copy, scale=gates[:, PACK + t : PACK + t + 1])
+        haar((2, 3), sb("neg_pa23", [P, 2, W], F32, tag="wb_grouped"))
+        z2_grouped = sb("z2_grouped", [P, D, PACK], BF16)
+        for h in range(2):
+            nc.scalar.copy(
+                lines(z2_grouped[:, h * W : (h + 1) * W, :], "p (c i) j -> p c j i"),
+                lines(z2_planes[:, :, h * W : (h + 1) * W], "p j (c i) -> p c j i"),
+            )
+        z_planes = sb("z_planes", [P, PACK, D], BF16, tag="planes")
+        for t in range(PACK):
+            nc.scalar.activation(
+                z_planes[:, t, :].rearrange("p (u m) -> p m u", u=PACK),
+                dt[t][:].rearrange("p (m u) -> p m u", u=PACK),
+                ACT.Copy,
+                scale=gates[:, t : t + 1],
+            )
+        z2_words = sb("z2_words", [P, D], U32)
+        z2_scales = sb("z2_scales", [P, D], U8)
+        quantize(z2_words, z2_scales, z2_grouped, 0, D)
+
+        z_grouped = sb("z_grouped", [P, D, PACK], BF16)
+        z_words = sb("z_words", [P, D], U32)
+        z_scales = sb("z_scales", [P, D], U8)
+        for pair in ((0, 1), (2, 3)):
+            for u in pair:
+                nc.vector.tensor_copy(
+                    lines(z_grouped[:, u * P : (u + 1) * P, :], "p (c i) j -> p c j i"),
+                    lines(z_planes[:, :, u * P : (u + 1) * P], "p j (c i) -> p c j i"),
+                )
+            for u in pair:
+                quantize(z_words, z_scales, z_grouped, u * P, (u + 1) * P)
+
+        cv = []
+        cv_again = []
+        for u in range(PACK):
+            acc = psum.tile([P, D], F32, name="acc", tag="acc")
+            mx(acc, z_words, z_scales, u, z2_words, z2_scales)
+            window = sb(f"cv{u}", [P, D], F32)
+            nc.scalar.activation(window[:], acc[:], ACT.Copy, scale=0.0625)
+            again = sb(f"cv_again{u}", [P, D], F32)
+            if u < 2:
+                nc.vector.tensor_copy(again[:], window[:])
+            else:
+                nc.scalar.activation(again[:], acc[:], ACT.Copy, scale=0.0625)
+            cv.append(window)
+            cv_again.append(again)
+
+        y_words = sb("y_words", [P, D], U32)
+        y_scales = sb("y_scales", [P, D], U8)
+        y_grouped = sb("y_grouped", [P, D, PACK], BF16)
+        out_rows = out_0.rearrange("(p u) c -> p u c", u=PACK)
+        out_words = out_1[0].rearrange("p c r -> p (c r)").bitcast(I32)
+        for h in range(2):
+            cols = slice(h * W, (h + 1) * W)
+            entries = slice(h * W // 16, (h + 1) * W // 16)
+            neg_diff = sb(f"neg_diff{h}", [P, PACK, W], F32)
+            gate = sb(f"gate{h}", [P, PACK, W], F32)
+            y = sb(f"y{h}", [P, PACK, W], F32)
+            for u in range(PACK):
+                nc.scalar.activation(gate[:, u, :], cv[u][:].indirect(n4_l[:, entries]), ACT.Sigmoid)
+                nc.vector.tensor_tensor(
+                    neg_diff[:, u, :], cv[u][:].indirect(n3_l[:, entries]), cv_again[u][:, cols], ALU.subtract
+                )
+            for u in range(PACK):
+                nc.vector.scalar_tensor_tensor(y[:, u, :], neg_diff[:, u, :], -1.0, gate[:, u, :], ALU.mult, ALU.mult)
+            nc.sync.dma_start(out_rows[:, :, cols], y[:])
+            nc.vector.tensor_copy(
+                lines(y_grouped[:, cols, :], "p (c i) j -> p c j i"), lines(y[:], "p j (c i) -> p c j i")
+            )
+            quantize(y_words, y_scales, y_grouped, h * W, (h + 1) * W)
+            nc.sync.dma_start(out_words[:, cols], y_words[:, cols].bitcast(I32))
+        for q in range(QUADS):
+            queue = nc.sync if q % 2 == 0 else nc.scalar
+            queue.dma_start(out_2[0, 4 * q : 4 * q + 4, :].bitcast(I32), y_scales[32 * q : 32 * q + 4, :].bitcast(I32))

@@ -28,7 +28,8 @@ def tile_picked_momhaargdif_none_po_kernel(
     nc = tc.nc
     with ExitStack() as ctx:
         keep = ctx.enter_context(tc.tile_pool(name="keep", bufs=1))
-        psum = ctx.enter_context(tc.psum_pool(name="psum", bufs=4))
+        psum = ctx.enter_context(tc.psum_pool(name="psum", bufs=7))
+        psum_once = ctx.enter_context(tc.psum_pool(name="psum_once", bufs=1))
 
         def sb(name, shape, dtype, tag=None):
             return keep.tile(shape, dtype, name=name, tag=tag or name, align_bytes=64)
@@ -43,14 +44,14 @@ def tile_picked_momhaargdif_none_po_kernel(
             nc.sync.dma_start(tile[:], w.rearrange("(p j) c -> p j c", j=PACK)[:, :, h * W : (h + 1) * W])
             return tile
 
-        def mx(out, lhs_words, lhs_scales, t, rhs_words, rhs_scales):
+        def mx(out, lhs_words, lhs_scales, t, rhs_words, rhs_scales, c0=0, c1=D):
             cols = slice(t * P, (t + 1) * P)
             nc.tensor.matmul_mx(
-                out=out[:],
+                out=out[:, c0:c1],
                 lhsT=lhs_words[:, cols].bitcast(FP8X4),
                 lhsT_scale=lhs_scales[:, cols],
-                rhs=rhs_words[:].bitcast(FP8X4),
-                rhs_scale=rhs_scales[:],
+                rhs=rhs_words[:, c0:c1].bitcast(FP8X4),
+                rhs_scale=rhs_scales[:, c0:c1],
                 start=True,
                 stop=True,
             )
@@ -66,7 +67,7 @@ def tile_picked_momhaargdif_none_po_kernel(
             return ap.rearrange(pattern, i=4)
 
         xs = sb("xs", [P, T], U8)
-        nc.vector.memset(xs[:].bitcast(I32), 0)
+        nc.gpsimd.memset(xs[:].bitcast(I32), 0)
         gate_rows = sb("gate_rows", [P, P], F32)
         nc.gpsimd.memset(gate_rows[:], 0.0)
         factor = sb("factor", [P, W], F32)
@@ -85,7 +86,7 @@ def tile_picked_momhaargdif_none_po_kernel(
         wa_raw = [load_weight_half(f"wa_raw{h}", wa, h) for h in range(2)]
         n1_l = load_list("n1_l", n1)
         n2_l = load_list("n2_l", n2)
-        for g, vec in enumerate((gt, gi)):
+        for g, vec in enumerate((gi, gt)):
             nc.sync.dma_start(
                 gate_rows[PACK * g : PACK * (g + 1), :].rearrange("t (b r) -> t b r", r=8),
                 vec.rearrange("(b t r) o -> t b (r o)", t=PACK, r=8),
@@ -104,8 +105,8 @@ def tile_picked_momhaargdif_none_po_kernel(
             )
             return dealt
 
-        def pick_words(name, lst):
-            dealt = sb(name, [P, D], U32)
+        def pick_words(name, lst, tag=None):
+            dealt = sb(name, [P, D], U32, tag=tag)
             nc.vector.tensor_copy(
                 dealt[:].rearrange("p (t b r) -> p b t r", t=PACK, r=8), xw[:].bitcast(U32).indirect(lst[:])
             )
@@ -123,7 +124,6 @@ def tile_picked_momhaargdif_none_po_kernel(
         xa_scales = pick_scales("xa_scales", offs_l)
         xb_scales = pick_scales("xb_scales", two_l)
         xa_words = pick_words("xa_words", offs_l)
-        xb_words = pick_words("xb_words", two_l)
         wa_grouped = sb("wa_grouped", [P, D, PACK], BF16)
         wa_words = sb("wa_words", [P, D], U32)
         wa_scales = sb("wa_scales", [P, D], U8)
@@ -138,88 +138,97 @@ def tile_picked_momhaargdif_none_po_kernel(
             )
         for h in range(2):
             quantize(wa_words, wa_scales, wa_grouped, h * W, (h + 1) * W)
+        xb_words = pick_words("xb_words", two_l, tag="wa_grouped")
 
-        neg_a = []
-        for t in range(PACK):
-            acc = psum.tile([P, D], F32, name="acc", tag="acc")
-            mx(acc, xa_words, xa_scales, t, wa_words, wa_scales)
-            window = sb(f"neg_a{t}", [P, D], F32)
-            nc.scalar.activation(window[:], acc[:], ACT.Copy, scale=-1.0)
-            neg_a.append(window)
+        neg_a = [sb(f"neg_a{t}", [P, D], F32) for t in range(PACK)]
+        for pair in ((0, 1), (2, 3)):
+            for h in range(2):
+                for t in pair:
+                    acc = psum.tile([P, W], F32, name="acc", tag="acc")
+                    mx(acc, xa_words, xa_scales, t, wa_words[:, h * W : (h + 1) * W], wa_scales[:, h * W : (h + 1) * W], 0, W)
+                    nc.scalar.activation(neg_a[t][:, h * W : (h + 1) * W], acc[:], ACT.Copy, scale=-1.0)
 
-        turned = psum.tile([P, P], F32, name="turned", tag="side")
+        turned = psum_once.tile([P, P], F32, name="turned")
         nc.tensor.transpose(turned[:], gate_rows[:], ident[:])
-        gates = sb("gates", [P, 2 * PACK], F32)
-        nc.scalar.copy(gates[:], turned[:, 0 : 2 * PACK])
+        gates = sb("gates", [P, 6], F32)
+        nc.scalar.copy(gates[:], turned[:, 0:6])
 
         z2_planes = sb("z2_planes", [P, PACK, D], BF16, tag="planes")
         neg_sum = [sb(f"neg_sum{t}", [P, W], F32) for t in range(PACK)]
-        two_pa = [sb(f"two_pa{t}", [P, W], F32) for t in range(PACK)]
         dt = [sb(f"dt{t}", [P, D], F32) for t in range(PACK)]
 
         def haar(pair, neg_pa):
             for t in pair:
                 nc.vector.tensor_copy(neg_pa[:, t % 2, :], neg_a[t][:].indirect(n1_l[:]))
-                nc.scalar.activation(two_pa[t][:], neg_pa[:, t % 2, :], ACT.Copy, scale=-2.0)
+            two_pa = sb(f"two_pa{pair[0]}", [P, 2, W], F32)
+            nc.scalar.activation(two_pa[:], neg_pa[:], ACT.Copy, scale=-2.0)
             for t in pair:
                 nc.vector.tensor_tensor(neg_sum[t][:], neg_a[t][:].indirect(n2_l[:]), neg_pa[:, t % 2, :], ALU.add)
             for t in pair:
                 nc.vector.tensor_tensor(dt[t][:].indirect(n1_l[:]), neg_sum[t][:], factor[:], ALU.mult)
             for t in pair:
-                nc.vector.tensor_tensor(dt[t][:].indirect(n2_l[:]), neg_sum[t][:], two_pa[t][:], ALU.add)
+                nc.vector.tensor_tensor(dt[t][:].indirect(n2_l[:]), neg_sum[t][:], two_pa[:, t % 2, :], ALU.add)
+
+        def weigh(t, gate, u0, u1):
+            nc.scalar.activation(
+                z_grouped[:, u0 * P : u1 * P, t].rearrange("p (u m) -> p u m", m=P),
+                dt[t][:].rearrange("p (m u) -> p u m", u=PACK)[:, u0:u1, :],
+                ACT.Copy,
+                scale=gate,
+            )
 
         haar((0, 1), sb("neg_pa01", [P, 2, W], F32))
         wb_grouped = group_weight("wb_grouped", wb_raw)
+        z_grouped = sb("z_grouped", [P, D, PACK], BF16, tag="wb_raw1")
+        for t in range(2):
+            weigh(t, gates[:, PACK + t : PACK + t + 1], 0, PACK)
         wb_words = sb("wb_words", [P, D], U32)
         wb_scales = sb("wb_scales", [P, D], U8)
         quantize(wb_words, wb_scales, wb_grouped, 0, D)
-        for t in range(PACK):
-            side = psum.tile([P, D], F32, name="side", tag="side")
-            mx(side, xb_words, xb_scales, t, wb_words, wb_scales)
-            nc.scalar.activation(z2_planes[:, t, :], side[:], ACT.Copy, scale=gates[:, PACK + t : PACK + t + 1])
         haar((2, 3), sb("neg_pa23", [P, 2, W], F32, tag="wb_grouped"))
+        for t in range(PACK):
+            side = psum.tile([P, D], F32, name="side", tag="acc")
+            mx(side, xb_words, xb_scales, t, wb_words, wb_scales)
+            nc.scalar.activation(z2_planes[:, t, :], side[:], ACT.Copy, scale=gates[:, t : t + 1])
         z2_grouped = sb("z2_grouped", [P, D, PACK], BF16)
         for h in range(2):
             nc.scalar.copy(
                 lines(z2_grouped[:, h * W : (h + 1) * W, :], "p (c i) j -> p c j i"),
                 lines(z2_planes[:, :, h * W : (h + 1) * W], "p j (c i) -> p c j i"),
             )
-        z_planes = sb("z_planes", [P, PACK, D], BF16, tag="planes")
-        for t in range(PACK):
-            nc.scalar.activation(
-                z_planes[:, t, :].rearrange("p (u m) -> p m u", u=PACK),
-                dt[t][:].rearrange("p (m u) -> p m u", u=PACK),
-                ACT.Copy,
-                scale=gates[:, t : t + 1],
-            )
+        late_gates = sb("late_gates", [P, 2], F32, tag="planes")
+        nc.scalar.copy(late_gates[:], turned[:, 6:8])
+        weigh(2, late_gates[:, 0:1], 0, PACK)
         z2_words = sb("z2_words", [P, D], U32)
         z2_scales = sb("z2_scales", [P, D], U8)
         quantize(z2_words, z2_scales, z2_grouped, 0, D)
 
-        z_grouped = sb("z_grouped", [P, D, PACK], BF16)
         z_words = sb("z_words", [P, D], U32)
         z_scales = sb("z_scales", [P, D], U8)
-        for pair in ((0, 1), (2, 3)):
-            for u in pair:
-                nc.vector.tensor_copy(
-                    lines(z_grouped[:, u * P : (u + 1) * P, :], "p (c i) j -> p c j i"),
-                    lines(z_planes[:, :, u * P : (u + 1) * P], "p j (c i) -> p c j i"),
-                )
-            for u in pair:
-                quantize(z_words, z_scales, z_grouped, u * P, (u + 1) * P)
+        for u in range(PACK):
+            weigh(3, late_gates[:, 1:2], u, u + 1)
+            quantize(z_words, z_scales, z_grouped, u * P, (u + 1) * P)
 
         cv = []
         cv_again = []
         for u in range(PACK):
-            acc = psum.tile([P, D], F32, name="acc", tag="acc")
-            mx(acc, z_words, z_scales, u, z2_words, z2_scales)
             window = sb(f"cv{u}", [P, D], F32)
-            nc.scalar.activation(window[:], acc[:], ACT.Copy, scale=0.0625)
             again = sb(f"cv_again{u}", [P, D], F32)
-            if u < 2:
-                nc.vector.tensor_copy(again[:], window[:])
+            if u == 0:
+                for h in range(2):
+                    cols = slice(h * W, (h + 1) * W)
+                    acc = psum.tile([P, W], F32, name="acc", tag="acc")
+                    mx(acc, z_words, z_scales, u, z2_words[:, cols], z2_scales[:, cols], 0, W)
+                    nc.scalar.activation(window[:, cols], acc[:], ACT.Copy, scale=0.0625)
+                    nc.vector.tensor_copy(again[:, cols], window[:, cols])
             else:
-                nc.scalar.activation(again[:], acc[:], ACT.Copy, scale=0.0625)
+                acc = psum.tile([P, D], F32, name="acc", tag="acc")
+                mx(acc, z_words, z_scales, u, z2_words, z2_scales)
+                nc.scalar.activation(window[:], acc[:], ACT.Copy, scale=0.0625)
+                if u < 3:
+                    nc.vector.tensor_copy(again[:], window[:])
+                else:
+                    nc.scalar.activation(again[:], acc[:], ACT.Copy, scale=0.0625)
             cv.append(window)
             cv_again.append(again)
 
@@ -228,23 +237,29 @@ def tile_picked_momhaargdif_none_po_kernel(
         y_grouped = sb("y_grouped", [P, D, PACK], BF16)
         out_rows = out_0.rearrange("(p u) c -> p u c", u=PACK)
         out_words = out_1[0].rearrange("p c r -> p (c r)").bitcast(I32)
+        gate = [sb(f"gate{h}", [P, PACK, W], F32) for h in range(2)]
+        y = [sb(f"y{h}", [P, PACK, W], F32) for h in range(2)]
         for h in range(2):
             cols = slice(h * W, (h + 1) * W)
             entries = slice(h * W // 16, (h + 1) * W // 16)
             neg_diff = sb(f"neg_diff{h}", [P, PACK, W], F32)
-            gate = sb(f"gate{h}", [P, PACK, W], F32)
-            y = sb(f"y{h}", [P, PACK, W], F32)
             for u in range(PACK):
-                nc.scalar.activation(gate[:, u, :], cv[u][:].indirect(n4_l[:, entries]), ACT.Sigmoid)
+                nc.scalar.activation(gate[h][:, u, :], cv[u][:].indirect(n4_l[:, entries]), ACT.Sigmoid)
                 nc.vector.tensor_tensor(
                     neg_diff[:, u, :], cv[u][:].indirect(n3_l[:, entries]), cv_again[u][:, cols], ALU.subtract
                 )
             for u in range(PACK):
-                nc.vector.scalar_tensor_tensor(y[:, u, :], neg_diff[:, u, :], -1.0, gate[:, u, :], ALU.mult, ALU.mult)
-            nc.sync.dma_start(out_rows[:, :, cols], y[:])
-            nc.vector.tensor_copy(
-                lines(y_grouped[:, cols, :], "p (c i) j -> p c j i"), lines(y[:], "p j (c i) -> p c j i")
+                nc.vector.scalar_tensor_tensor(
+                    y[h][:, u, :], neg_diff[:, u, :], -1.0, gate[h][:, u, :], ALU.mult, ALU.mult
+                )
+            nc.sync.dma_start(out_rows[:, :, cols], y[h][:])
+        for h, copy in enumerate((nc.scalar.copy, nc.vector.tensor_copy)):
+            copy(
+                lines(y_grouped[:, h * W : (h + 1) * W, :], "p (c i) j -> p c j i"),
+                lines(y[h][:], "p j (c i) -> p c j i"),
             )
+        for h in range(2):
+            cols = slice(h * W, (h + 1) * W)
             quantize(y_words, y_scales, y_grouped, h * W, (h + 1) * W)
             nc.sync.dma_start(out_words[:, cols], y_words[:, cols].bitcast(I32))
         for q in range(QUADS):

from contextlib import ExitStack

import concourse.mybir as mybir
from concourse.masks import make_identity

F32 = mybir.dt.float32
BF16 = mybir.dt.bfloat16
U32 = mybir.dt.uint32
I32 = mybir.dt.int32
U16 = mybir.dt.uint16
U8 = mybir.dt.uint8
FP8X4 = mybir.dt.float8_e4m3fn_x4
ALU = mybir.AluOpType
ACT = mybir.ActivationFunctionType

P = 128
PACK = 4
T = 2048
D = 512
W = 256
QUADS = 4
FLOPS = 3 * 2 * D * D * D


def tile_picked_momhaargdif_none_po_kernel(
    tc, x_words, x_scales, wa, wb, gt, gi, offs, two, n1, n2, n3, n4, out_0, out_1, out_2
):
    nc = tc.nc
    with ExitStack() as ctx:
        keep = ctx.enter_context(tc.tile_pool(name="keep", bufs=1))
        psum = ctx.enter_context(tc.psum_pool(name="psum", bufs=7))
        psum_once = ctx.enter_context(tc.psum_pool(name="psum_once", bufs=1))

        def sb(name, shape, dtype, tag=None):
            return keep.tile(shape, dtype, name=name, tag=tag or name, align_bytes=64)

        def load_list(name, src):
            tile = sb(name, list(src.shape), U16)
            nc.sync.dma_start(tile[:], src)
            return tile

        def load_weight_half(name, w, h):
            tile = sb(name, [P, PACK, W], F32)
            nc.sync.dma_start(tile[:], w.rearrange("(p j) c -> p j c", j=PACK)[:, :, h * W : (h + 1) * W])
            return tile

        def mx(out, lhs_words, lhs_scales, t, rhs_words, rhs_scales, c0=0, c1=D):
            cols = slice(t * P, (t + 1) * P)
            nc.tensor.matmul_mx(
                out=out[:, c0:c1],
                lhsT=lhs_words[:, cols].bitcast(FP8X4),
                lhsT_scale=lhs_scales[:, cols],
                rhs=rhs_words[:, c0:c1].bitcast(FP8X4),
                rhs_scale=rhs_scales[:, c0:c1],
                start=True,
                stop=True,
            )

        def quantize(words, scales, grouped, c0, c1):
            nc.vector.quantize_mx(
                out=words[:, c0:c1].bitcast(FP8X4),
                scales=scales[:, c0:c1],
                in_=grouped[:, c0:c1, :].rearrange("p c j -> p (c j)"),
            )

        def lines(ap, pattern):
            return ap.rearrange(pattern, i=4)

        xs = sb("xs", [P, T], U8)
        nc.gpsimd.memset(xs[:].bitcast(I32), 0)
        gate_rows = sb("gate_rows", [P, P], F32)
        nc.gpsimd.memset(gate_rows[:], 0.0)
        factor = sb("factor", [P, W], F32)
        nc.gpsimd.memset(factor[:], -0.75)
        ident = sb("ident", [P, P], F32)
        make_identity(nc, ident[:])

        offs_l = load_list("offs_l", offs)
        two_l = load_list("two_l", two)
        for q in range(QUADS):
            nc.sync.dma_start(xs[32 * q : 32 * q + 4, :].bitcast(I32), x_scales[0, 4 * q : 4 * q + 4, :].bitcast(I32))
        warm = sb("warm", [P, 1], F32)
        nc.scalar.activation(warm[:], factor[:, 0:1], ACT.Sigmoid)
        xw = sb("xw", [P, T], I32)
        nc.sync.dma_start(xw[:], x_words[0].rearrange("p n r -> p (n r)").bitcast(I32))
        wa_raw = [load_weight_half(f"wa_raw{h}", wa, h) for h in range(2)]
        n1_l = load_list("n1_l", n1)
        n2_l = load_list("n2_l", n2)
        for g, vec in enumerate((gi, gt)):
            nc.sync.dma_start(
                gate_rows[PACK * g : PACK * (g + 1), :].rearrange("t (b r) -> t b r", r=8),
                vec.rearrange("(b t r) o -> t b (r o)", t=PACK, r=8),
            )
        wb_raw = [load_weight_half(f"wb_raw{h}", wb, h) for h in range(2)]
        n3_l = load_list("n3_l", n3)
        n4_l = load_list("n4_l", n4)

        def pick_scales(name, lst):
            picked = sb(name + "_picked", [P, D], U8)
            nc.vector.tensor_copy(picked[:], xs[:].indirect(lst[:]))
            dealt = sb(name, [P, D], U8)
            nc.vector.tensor_copy(
                dealt[:].bitcast(I32).rearrange("p (t b w) -> p t b w", t=PACK, w=2),
                picked[:].bitcast(I32).rearrange("p (b t w) -> p t b w", t=PACK, w=2),
            )
            return dealt

        def pick_words(name, lst, tag=None):
            dealt = sb(name, [P, D], U32, tag=tag)
            nc.vector.tensor_copy(
                dealt[:].rearrange("p (t b r) -> p b t r", t=PACK, r=8), xw[:].bitcast(U32).indirect(lst[:])
            )
            return dealt

        def group_weight(name, raw):
            grouped = sb(name, [P, D, PACK], BF16)
            for h in range(2):
                nc.scalar.copy(
                    lines(grouped[:, h * W : (h + 1) * W, :], "p (c i) j -> p c j i"),
                    lines(raw[h][:], "p j (c i) -> p c j i"),
                )
            return grouped

        xa_scales = pick_scales("xa_scales", offs_l)
        xb_scales = pick_scales("xb_scales", two_l)
        xa_words = pick_words("xa_words", offs_l)
        wa_grouped = sb("wa_grouped", [P, D, PACK], BF16)
        wa_words = sb("wa_words", [P, D], U32)
        wa_scales = sb("wa_scales", [P, D], U8)
        for copy, h, c0, c1 in (
            (nc.scalar.copy, 0, 0, W),
            (nc.scalar.copy, 1, 0, P),
            (nc.vector.tensor_copy, 1, P, W),
        ):
            copy(
                lines(wa_grouped[:, h * W + c0 : h * W + c1, :], "p (c i) j -> p c j i"),
                lines(wa_raw[h][:, :, c0:c1], "p j (c i) -> p c j i"),
            )
        for h in range(2):
            quantize(wa_words, wa_scales, wa_grouped, h * W, (h + 1) * W)
        xb_words = pick_words("xb_words", two_l, tag="wa_grouped")

        neg_a = [sb(f"neg_a{t}", [P, D], F32) for t in range(PACK)]
        for pair in ((0, 1), (2, 3)):
            for h in range(2):
                for t in pair:
                    acc = psum.tile([P, W], F32, name="acc", tag="acc")
                    mx(acc, xa_words, xa_scales, t, wa_words[:, h * W : (h + 1) * W], wa_scales[:, h * W : (h + 1) * W], 0, W)
                    nc.scalar.activation(neg_a[t][:, h * W : (h + 1) * W], acc[:], ACT.Copy, scale=-1.0)

        turned = psum_once.tile([P, P], F32, name="turned")
        nc.tensor.transpose(turned[:], gate_rows[:], ident[:])
        gates = sb("gates", [P, 6], F32)
        nc.scalar.copy(gates[:], turned[:, 0:6])

        z2_planes = sb("z2_planes", [P, PACK, D], BF16, tag="planes")
        neg_sum = [sb(f"neg_sum{t}", [P, W], F32) for t in range(PACK)]
        dt = [sb(f"dt{t}", [P, D], F32) for t in range(PACK)]

        def haar(pair, neg_pa):
            for t in pair:
                nc.vector.tensor_copy(neg_pa[:, t % 2, :], neg_a[t][:].indirect(n1_l[:]))
            two_pa = sb(f"two_pa{pair[0]}", [P, 2, W], F32)
            nc.scalar.activation(two_pa[:], neg_pa[:], ACT.Copy, scale=-2.0)
            for t in pair:
                nc.vector.tensor_tensor(neg_sum[t][:], neg_a[t][:].indirect(n2_l[:]), neg_pa[:, t % 2, :], ALU.add)
            for t in pair:
                nc.vector.tensor_tensor(dt[t][:].indirect(n1_l[:]), neg_sum[t][:], factor[:], ALU.mult)
            for t in pair:
                nc.vector.tensor_tensor(dt[t][:].indirect(n2_l[:]), neg_sum[t][:], two_pa[:, t % 2, :], ALU.add)

        def weigh(t, gate, u0, u1):
            nc.scalar.activation(
                z_grouped[:, u0 * P : u1 * P, t].rearrange("p (u m) -> p u m", m=P),
                dt[t][:].rearrange("p (m u) -> p u m", u=PACK)[:, u0:u1, :],
                ACT.Copy,
                scale=gate,
            )

        haar((0, 1), sb("neg_pa01", [P, 2, W], F32))
        wb_grouped = group_weight("wb_grouped", wb_raw)
        z_grouped = sb("z_grouped", [P, D, PACK], BF16, tag="wb_raw1")
        for t in range(2):
            weigh(t, gates[:, PACK + t : PACK + t + 1], 0, PACK)
        wb_words = sb("wb_words", [P, D], U32)
        wb_scales = sb("wb_scales", [P, D], U8)
        quantize(wb_words, wb_scales, wb_grouped, 0, D)
        haar((2, 3), sb("neg_pa23", [P, 2, W], F32, tag="wb_grouped"))
        for t in range(PACK):
            side = psum.tile([P, D], F32, name="side", tag="acc")
            mx(side, xb_words, xb_scales, t, wb_words, wb_scales)
            nc.scalar.activation(z2_planes[:, t, :], side[:], ACT.Copy, scale=gates[:, t : t + 1])
        z2_grouped = sb("z2_grouped", [P, D, PACK], BF16)
        for h in range(2):
            nc.scalar.copy(
                lines(z2_grouped[:, h * W : (h + 1) * W, :], "p (c i) j -> p c j i"),
                lines(z2_planes[:, :, h * W : (h + 1) * W], "p j (c i) -> p c j i"),
            )
        late_gates = sb("late_gates", [P, 2], F32, tag="planes")
        nc.scalar.copy(late_gates[:], turned[:, 6:8])
        weigh(2, late_gates[:, 0:1], 0, PACK)
        z2_words = sb("z2_words", [P, D], U32)
        z2_scales = sb("z2_scales", [P, D], U8)
        quantize(z2_words, z2_scales, z2_grouped, 0, D)

        z_words = sb("z_words", [P, D], U32)
        z_scales = sb("z_scales", [P, D], U8)
        for u in range(PACK):
            weigh(3, late_gates[:, 1:2], u, u + 1)
            quantize(z_words, z_scales, z_grouped, u * P, (u + 1) * P)

        cv = []
        cv_again = []
        for u in range(PACK):
            window = sb(f"cv{u}", [P, D], F32)
            again = sb(f"cv_again{u}", [P, D], F32)
            if u == 0:
                for h in range(2):
                    cols = slice(h * W, (h + 1) * W)
                    acc = psum.tile([P, W], F32, name="acc", tag="acc")
                    mx(acc, z_words, z_scales, u, z2_words[:, cols], z2_scales[:, cols], 0, W)
                    nc.scalar.activation(window[:, cols], acc[:], ACT.Copy, scale=0.0625)
                    nc.vector.tensor_copy(again[:, cols], window[:, cols])
            else:
                acc = psum.tile([P, D], F32, name="acc", tag="acc")
                mx(acc, z_words, z_scales, u, z2_words, z2_scales)
                nc.scalar.activation(window[:], acc[:], ACT.Copy, scale=0.0625)
                if u < 3:
                    nc.vector.tensor_copy(again[:], window[:])
                else:
                    nc.scalar.activation(again[:], acc[:], ACT.Copy, scale=0.0625)
            cv.append(window)
            cv_again.append(again)

        y_words = sb("y_words", [P, D], U32)
        y_scales = sb("y_scales", [P, D], U8)
        y_grouped = sb("y_grouped", [P, D, PACK], BF16)
        out_rows = out_0.rearrange("(p u) c -> p u c", u=PACK)
        out_words = out_1[0].rearrange("p c r -> p (c r)").bitcast(I32)
        gate = [sb(f"gate{h}", [P, PACK, W], F32) for h in range(2)]
        y = [sb(f"y{h}", [P, PACK, W], F32) for h in range(2)]
        for h in range(2):
            cols = slice(h * W, (h + 1) * W)
            entries = slice(h * W // 16, (h + 1) * W // 16)
            neg_diff = sb(f"neg_diff{h}", [P, PACK, W], F32)
            for u in range(PACK):
                nc.scalar.activation(gate[h][:, u, :], cv[u][:].indirect(n4_l[:, entries]), ACT.Sigmoid)
                nc.vector.tensor_tensor(
                    neg_diff[:, u, :], cv[u][:].indirect(n3_l[:, entries]), cv_again[u][:, cols], ALU.subtract
                )
            for u in range(PACK):
                nc.vector.scalar_tensor_tensor(
                    y[h][:, u, :], neg_diff[:, u, :], -1.0, gate[h][:, u, :], ALU.mult, ALU.mult
                )
            nc.sync.dma_start(out_rows[:, :, cols], y[h][:])
        for h, copy in enumerate((nc.scalar.copy, nc.vector.tensor_copy)):
            copy(
                lines(y_grouped[:, h * W : (h + 1) * W, :], "p (c i) j -> p c j i"),
                lines(y[h][:], "p j (c i) -> p c j i"),
            )
        for h in range(2):
            cols = slice(h * W, (h + 1) * W)
            quantize(y_words, y_scales, y_grouped, h * W, (h + 1) * W)
            nc.sync.dma_start(out_words[:, cols], y_words[:, cols].bitcast(I32))
        for q in range(QUADS):
            queue = nc.sync if q % 2 == 0 else nc.scalar
            queue.dma_start(out_2[0, 4 * q : 4 * q + 4, :].bitcast(I32), y_scales[32 * q : 32 * q + 4, :].bitcast(I32))
